import numpy as np
import ml_dtypes


def mxq(x, axis, fmt="e4m3"):
    dtype, down = {"e4m3": (ml_dtypes.float8_e4m3fn, 7), "e5m2": (ml_dtypes.float8_e5m2, 14)}[fmt]
    v = np.moveaxis(np.asarray(x, np.float32).astype(ml_dtypes.bfloat16).astype(np.float64), axis, -1)
    blocks = v.reshape(v.shape[:-1] + (-1, 32))
    amax = np.abs(blocks).max(-1, keepdims=True)
    byte = np.maximum(np.where(amax > 0, np.frexp(amax)[1] - 1 + 127, 0) - down, 1)
    scale = np.exp2(byte - 127.0)
    codes = (blocks / scale).astype(np.float32).astype(dtype).astype(np.float64)
    return np.moveaxis((codes * scale).reshape(v.shape), -1, axis)


WIDE = False


def mx_kscale(k):
    if not WIDE:
        return np.ones(k)
    levels = np.array([30, -30])
    if k % 512:
        return np.exp2(np.random.permutation(np.resize(levels, k // 32))).repeat(32)
    a = np.empty((k // 512, 16))
    for p in range(k // 512):
        a[p, :8] = np.random.permutation(np.resize(levels, 8))
        for g in range(8):
            far = levels[np.abs(levels - a[p, g]) >= 10]
            a[p, g + 8] = far[np.random.randint(len(far))]
    return np.exp2(a.ravel()).repeat(32)


BF16 = ml_dtypes.bfloat16


def bf(x):
    return np.asarray(x, np.float32).astype(BF16)


def f64(x):
    return np.asarray(x).astype(np.float64)


E2M1 = np.array([0.0, 0.5, 1.0, 1.5, 2.0, 3.0, 4.0, 6.0, -0.0, -0.5, -1.0, -1.5, -2.0, -3.0, -4.0, -6.0])


def pack_weight(w, fmt):
    k, n = w.shape
    w = f64(bf(w)).reshape(k // 32, 32, n)
    amax = np.abs(w).max(1)
    if fmt in ("e4m3", "e5m2"):
        byte = np.frexp(amax)[1] - 1 + 127 - (7 if fmt == "e4m3" else 14)
    else:
        mant, ex = np.frexp(amax / 6.0)
        byte = np.where(mant > 0.5, ex, ex - 1) + 127
    byte = np.clip(np.where(amax > 0, byte, 1), 1, 254)
    scaled = (w * np.exp2(127.0 - byte)[:, None, :]).reshape(k, n).astype(np.float32)
    by_word = np.ascontiguousarray(scaled.reshape(k // 512, 128, 4, n).transpose(0, 1, 3, 2))
    if fmt in ("e4m3", "e5m2"):
        words = by_word.astype(ml_dtypes.float8_e4m3fn if fmt == "e4m3" else ml_dtypes.float8_e5m2).view(np.uint8)
    else:
        c = by_word.astype(ml_dtypes.float4_e2m1fn).view(np.uint8) & 0xF
        words = c[..., 0::2] | (c[..., 1::2] << 4)
    return np.ascontiguousarray(words), np.ascontiguousarray(byte.astype(np.uint8).reshape(k // 512, 16, n))


def unpack_weight(words, scales, fmt):
    g, p, n, _ = words.shape
    if fmt in ("e4m3", "e5m2"):
        vals = np.ascontiguousarray(words).view(ml_dtypes.float8_e4m3fn if fmt == "e4m3" else ml_dtypes.float8_e5m2).astype(np.float64)
    else:
        nib = np.empty((g, p, n, 4), np.uint8)
        nib[..., 0::2] = words & 0xF
        nib[..., 1::2] = words >> 4
        vals = E2M1[nib]
    vals = vals * np.repeat(np.exp2(scales.astype(np.float64) - 127.0), 8, axis=1)[..., None]
    return vals.transpose(0, 1, 3, 2).reshape(g * 512, n)


S, D, B, C = 1024, 1536, 4, 384


def setup_inputs():
    s = mx_kscale(S)
    t = mx_kscale(D)
    G = np.random.standard_t(5, (S, B * C)) * s[:, None]
    G_words, G_scales = pack_weight(G, "e5m2")
    w2 = np.random.standard_normal((S, D)) / np.sqrt(S) / s[:, None] * t
    w1 = np.random.standard_normal((D, S)) / np.sqrt(D) / t[:, None]
    z = np.random.standard_normal((B, D, C))
    sg = 1.0 / (1.0 + np.exp(-z))
    return {"g_words": G_words, "g_scales": G_scales,
            "w2": bf(w2), "w1": bf(w1),
            "slope": bf(sg * (1.0 + z * (1.0 - sg))),
            "alpha": bf(1.0 + 0.1 * np.random.standard_normal(C)),
            "v": bf(np.random.uniform(0.5, 1.5, B))}


def reference(g_words, g_scales, w2, w1, slope, alpha, v):
    g = unpack_weight(g_words, g_scales, "e5m2")
    h = mxq(f64(w2), 0, "e4m3").T @ g
    p = h * f64(slope).transpose(1, 0, 2).reshape(D, B * C)
    r = mxq(f64(w1), 0, "e4m3").T @ mxq(p, 0, "e5m2")
    r = r.reshape(S, B, C).transpose(1, 0, 2)
    return r * f64(alpha) * f64(v)[:, None, None]

@@ -1,0 +1,190 @@
+from contextlib import ExitStack
+
+import concourse.mybir as mybir
+from concourse.masks import make_identity
+
+S, D, B, C = 1024, 1536, 4, 384
+NC = B * C
+FLOPS = 2 * 2 * S * D * NC
+
+F32 = mybir.dt.float32
+BF16 = mybir.dt.bfloat16
+U32 = mybir.dt.uint32
+I32 = mybir.dt.int32
+U8 = mybir.dt.uint8
+E4 = mybir.dt.float8_e4m3fn_x4
+E5 = mybir.dt.float8_e5m2_x4
+MULT = mybir.AluOpType.mult
+ADD = mybir.AluOpType.add
+P = 128
+
+LOADS = "Lw2_01 Lw2_00 Lw2_10 Lgs Lg0 Lsb0 Lsa0 Lw2_11 Lw2_20 Lw2_21 Lsa1 Lsb1 Lsb2 Lw1a1 Lw1a0 Lgs2 Lsa2 Lg1 Lsa3 Lsb3 Lsb4 Lsa4 Lw1a2 Lw1b1 Lsa5 Lw1b2 Lsb5 Lg2 Lw1b0 Lsb6 Lsa6 Lsa8 Lsa7 Lsb7 Lsb8"
+ORDER = "Vi2_0113 Si2_0101 q2_01 Si2_0001 Vi2_0012 Vi2_1021 Si2_1002 av Vi2_0031 q2_00 Vi2_1031 A00 q2_10 A01 A02 m00 A03 m01 m02 Si2_1102 Vi2_1122 m03 Si2_2002 q2_11 Vip002 Sip021 A10 Vi2_2101 A11 Si2_2021 Vi2_2031 Vi2_2111 A12 Si2_2122 q2_20 A13 m10 Si1_0101 q2_21 Si1_0001 m11 A20 m12 Sip031 A21 m13 Si1_0111 A22 m20 Si1_0011 A23 m21 Sip103 q1_00 A30 m22 A31 m23 A32 m30 Sip202 A33 m31 A40 m32 Sip131 A41 m33 Si1_0202 A42 q1_01 qp0 A43 Vip221 A50 Sip302 q1_02 A51 m40 A52 m41 Si1_1101 A53 Vip231 Si1_3101 qp1 Sip321 qp2 Si1_1111 m42 B00 Si1_1201 m43 m50 Si1_3202 m51 A60 m52 B01 Si1_3111 q1_11 Si1_2202 m53 A61 o00 A62 q1_31 Si1_3001 A63 Vi1_2101 q1_32 Sip501 A70 m60 A71 Si1_1211 o01 A72 Si1_1002 m61 A73 m62 A80 Si1_2001 m63 A81 q1_12 Si1_2111 q1_22 A82 q1_10 Sip511 m70 A83 Si1_2011 m71 B02 Si1_3011 m72 B03 Sip522 q1_21 q1_20 m73 B04 Sip401 m80 q1_30 B05 Sip331 qp5 Sip413 B06 m81 m82 B07 qp3 Sip601 m83 Sip701 qp4 o02 Sip801 B10 o03 Sip713 B11 o04 o05 B12 o06 Sip611 B13 o07 Sip813 o10 B14 o11 B15 o12 Sip622 qp7 B16 qp8 B17 qp6 o13 B20 o14 B21 o15 o16 B22 o17 B23 o20 o21 B24 o22 B25 o23 o24 B26 o25 B27 o26 o27"
+
+
+def pieces(n):
+    res = []
+    col = 512 * n
+    while col < 512 * (n + 1):
+        b = col // C
+        end = min((b + 1) * C, 512 * (n + 1))
+        res.append((b, col - b * C, end - b * C, col - 512 * n))
+        col = end
+    return res
+
+
+def tile_token_mixing_input_gradient_e3_kernel(tc, g_words, g_scales, w2, w1, slope, alpha, v, out):
+    nc = tc.nc
+    with ExitStack() as ctx:
+        keep = ctx.enter_context(tc.tile_pool(name="keep", bufs=1))
+        ring = ctx.enter_context(tc.tile_pool(name="ring", bufs=24))
+        psum = ctx.enter_context(tc.psum_pool(name="psum", bufs=8))
+        ctx.enter_context(tc.manual_schedule())
+
+        gs0 = keep.tile([P, 2, 512], U8, align_bytes=64)
+        gs12 = keep.tile([P, 2, 1024], U8, align_bytes=64)
+        nc.vector.memset(gs0[:].rearrange("p g n -> p (g n)").bitcast(I32), 0)
+        nc.vector.memset(gs12[:].rearrange("p g n -> p (g n)").bitcast(I32), 0)
+
+        cols = keep.tile([P, 16], F32)
+        nc.gpsimd.memset(cols[:], 0.0)
+        aw = alpha.bitcast(F32)
+        vw = v.bitcast(F32)
+        with nc.allow_non_contiguous_dma(reason="one word a partition"):
+            nc.gpsimd.dma_start(out=cols[:, 0:1], in_=aw[0:128].rearrange("(p o) -> p o", o=1))
+            nc.gpsimd.dma_start(out=cols[0:64, 8:9], in_=aw[128:192].rearrange("(p o) -> p o", o=1))
+            nc.gpsimd.dma_start(out=cols[64:66, 8:9], in_=vw.rearrange("(p o) -> p o", o=1))
+        ident = keep.tile([P, P], F32)
+        make_identity(nc, ident[:])
+        spread = psum.tile([P, 512], F32, name="bank")
+        nc.tensor.transpose(spread[:, 0:128], cols[:, 0:1].to_broadcast([P, P]), ident[:])
+        nc.tensor.transpose(spread[:, 128:256], cols[:, 8:9].to_broadcast([P, P]), ident[:])
+        avw = keep.tile([P, 256], F32)
+        av16 = avw[:].bitcast(BF16)
+
+        gw = keep.tile([P, 3, 2, 512], U32, align_bytes=64)
+        w2c = keep.tile([P, 2, D], U32, align_bytes=64)
+        w2s = keep.tile([P, 2, D], U8, align_bytes=64)
+        w1c = keep.tile([P, 3, S], U32, align_bytes=64)
+        w1s = keep.tile([P, 3, S], U8, align_bytes=64)
+        pc = keep.tile([P, 9, 512], U32, align_bytes=64)
+        psc = keep.tile([P, 9, 512], U8, align_bytes=64)
+        sl = keep.tile([P, 9, 4, 512], BF16)
+        w1a = keep.tile([P, 3, 4, 256], BF16)
+        w1b = keep.tile([P, 3, 4, 768], BF16)
+        tiles = {}
+
+        def buf(key, shape, dtype):
+            if key not in tiles:
+                fresh = ring.tile(shape, dtype, name="buf", align_bytes=64)
+                tiles[key] = fresh
+            return tiles[key]
+
+        def scale_rows(dst, c0, c1):
+            for q in range(4):
+                nc.sync.dma_start(out=dst[32 * q:32 * q + 4].bitcast(I32),
+                                  in_=g_scales[:, 4 * q:4 * q + 4, c0:c1].rearrange("g r n -> r g n").bitcast(I32))
+
+        for tok in LOADS.split():
+            if tok.startswith("Lw2_"):
+                c, g = int(tok[4]), int(tok[5])
+                raw = buf(("raw", c, g), [P, 4, 512], BF16)
+                nc.sync.dma_start(out=raw[:], in_=w2[512 * g:512 * (g + 1), 512 * c:512 * (c + 1)].rearrange("(p j) w -> p j w", j=4))
+            elif tok == "Lgs":
+                scale_rows(gs0, 0, 512)
+            elif tok == "Lgs2":
+                scale_rows(gs12, 512, NC)
+            elif tok.startswith("Lg"):
+                n = int(tok[2])
+                nc.sync.dma_start(out=gw[:, n].bitcast(I32),
+                                  in_=g_words[:, :, 512 * n:512 * (n + 1), :].rearrange("g p n t -> p g (n t)").bitcast(I32))
+            elif tok.startswith("Ls"):
+                k = int(tok[3])
+                n, c = divmod(k, 3)
+                b, c0, c1, off = pieces(n)[0 if tok[2] == "a" else 1]
+                nc.sync.dma_start(out=sl[:, k, :, off:off + c1 - c0],
+                                  in_=slope[b, 512 * c:512 * (c + 1), c0:c1].rearrange("(p t) x -> p t x", t=4))
+            elif tok.startswith("Lw1a"):
+                c = int(tok[4])
+                nc.sync.dma_start(out=w1a[:, c], in_=w1[512 * c:512 * (c + 1), 0:256].rearrange("(p j) w -> p j w", j=4))
+            else:
+                c = int(tok[4])
+                nc.sync.dma_start(out=w1b[:, c], in_=w1[512 * c:512 * (c + 1), 256:S].rearrange("(p j) w -> p j w", j=4))
+
+        def move(eng, dst, src):
+            if eng == "V":
+                nc.vector.tensor_copy(out=dst, in_=src)
+            elif eng == "S":
+                nc.scalar.copy(out=dst, in_=src)
+            else:
+                nc.gpsimd.tensor_scalar(out=dst, in0=src, scalar1=1.0, scalar2=0.0, op0=MULT, op1=ADD)
+
+        def interleave(eng, dst, src):
+            move(eng, dst.rearrange("p (x i j) -> p x j i", i=4, j=4), src.rearrange("p j (x i) -> p x j i", i=4))
+
+        def store(n, m0, cnt, res):
+            for (b, c0, c1, off) in pieces(n):
+                nc.sync.dma_start(out=out[b, 128 * m0:128 * (m0 + cnt), c0:c1].rearrange("(r p) x -> p r x", p=P),
+                                  in_=res[:, m0 % 2:m0 % 2 + cnt, off:off + c1 - c0])
+
+        for tok in ORDER.split():
+            if tok == "av":
+                nc.scalar.copy(out=avw[:], in_=spread[:, 0:256])
+            elif tok[1:].startswith("i2_"):
+                c, g, u, cnt = int(tok[4]), int(tok[5]), int(tok[6]), int(tok[7])
+                grp = buf(("g2", c, g), [P, 2048], BF16)
+                src = tiles[("raw", c, g)][:].rearrange("p j (m i t) -> p t m j i", i=2, t=4)
+                for t in range(u, u + cnt):
+                    move(tok[0], grp[:, 512 * t:512 * (t + 1)].rearrange("p (m i j) -> p m j i", i=2, j=4), src[:, t])
+            elif tok[1:].startswith("i1_"):
+                h, c, u, cnt = int(tok[4]), int(tok[5]), int(tok[6]), int(tok[7])
+                grp = buf(("g1", h, c), [P, 1024], BF16)
+                src = w1a[:, c] if h == 0 else w1b[:, c, :, 256 * (h - 1):256 * h]
+                interleave(tok[0], grp[:, 512 * u:512 * (u + cnt)], src[:, :, 128 * u:128 * (u + cnt)])
+            elif tok[1:].startswith("ip"):
+                k, u, cnt = int(tok[3]), int(tok[4]), int(tok[5])
+                grp = buf(("gp", k), [P, 2048], BF16)
+                interleave(tok[0], grp[:, 512 * u:512 * (u + cnt)], sl[:, k, :, 128 * u:128 * (u + cnt)])
+            elif tok.startswith("q2_"):
+                c, g = int(tok[3]), int(tok[4])
+                nc.vector.quantize_mx(out=w2c[:, g, 512 * c:512 * (c + 1)].bitcast(E4), scales=w2s[:, g, 512 * c:512 * (c + 1)],
+                                      in_=tiles[("g2", c, g)][:])
+            elif tok.startswith("q1_"):
+                h, c = int(tok[3]), int(tok[4])
+                nc.vector.quantize_mx(out=w1c[:, c, 256 * h:256 * (h + 1)].bitcast(E4), scales=w1s[:, c, 256 * h:256 * (h + 1)],
+                                      in_=tiles[("g1", h, c)][:])
+            elif tok.startswith("qp"):
+                k = int(tok[2])
+                nc.vector.quantize_mx(out=pc[:, k, :].bitcast(E5), scales=psc[:, k, :], in_=tiles[("gp", k)][:])
+            elif tok[0] == "A":
+                k, t = int(tok[1]), int(tok[2])
+                n, c = divmod(k, 3)
+                bank = psum.tile([P, 512], F32, name="bank")
+                tiles[tok[1:], "A"] = bank
+                mc = slice(512 * c + 128 * t, 512 * c + 128 * (t + 1))
+                for g in range(2):
+                    gsc = gs0[:, g, :] if n == 0 else gs12[:, g, 512 * (n - 1):512 * n]
+                    nc.tensor.matmul_mx(out=bank[:], lhsT=w2c[:, g, mc].bitcast(E4), lhsT_scale=w2s[:, g, mc],
+                                        rhs=gw[:, n, g, :].bitcast(E5), rhs_scale=gsc, start=(g == 0), stop=(g == 1))
+            elif tok[0] == "m":
+                k, t = int(tok[1]), int(tok[2])
+                nc.vector.tensor_tensor(out=sl[:, k, t, :], in0=tiles[tok[1:], "A"][:], in1=sl[:, k, t, :], op=MULT)
+            elif tok[0] == "B":
+                n, m = int(tok[1]), int(tok[2])
+                bank = psum.tile([P, 512], F32, name="bank")
+                tiles[tok[1:], "B"] = bank
+                mc = slice(128 * m, 128 * (m + 1))
+                for c in range(3):
+                    nc.tensor.matmul_mx(out=bank[:], lhsT=w1c[:, c, mc].bitcast(E4), lhsT_scale=w1s[:, c, mc],
+                                        rhs=pc[:, 3 * n + c, :].bitcast(E5), rhs_scale=psc[:, 3 * n + c, :], start=(c == 0), stop=(c == 2))
+            else:
+                n, m = int(tok[1]), int(tok[2])
+                res = buf(("res", n, m // 2), [P, 2, 512], F32)
+                bank = tiles[tok[1:], "B"]
+                for (b, c0, c1, off) in pieces(n):
+                    nc.vector.scalar_tensor_tensor(out=res[:, m % 2, off:off + c1 - c0], in0=bank[:, off:off + c1 - c0],
+                                                   scalar=av16[:, C + b:C + b + 1], in1=av16[:, c0:c1], op0=MULT, op1=MULT)
+                if n == 2 and m >= 6:
+                    store(n, m, 1, res)
+                elif m % 2 == 1:
+                    store(n, m - 1, 2, res)

@@ -16,10 +16,11 @@ E4 = mybir.dt.float8_e4m3fn_x4
 E5 = mybir.dt.float8_e5m2_x4
 MULT = mybir.AluOpType.mult
 ADD = mybir.AluOpType.add
+COPY = mybir.ActivationFunctionType.Copy
 P = 128
 
-LOADS = "Lw2_01 Lw2_00 Lw2_10 Lgs Lg0 Lsb0 Lsa0 Lw2_11 Lw2_20 Lw2_21 Lsa1 Lsb1 Lsb2 Lw1a1 Lw1a0 Lgs2 Lsa2 Lg1 Lsa3 Lsb3 Lsb4 Lsa4 Lw1a2 Lw1b1 Lsa5 Lw1b2 Lsb5 Lg2 Lw1b0 Lsb6 Lsa6 Lsa8 Lsa7 Lsb7 Lsb8"
-ORDER = "Vi2_0113 Si2_0101 q2_01 Si2_0001 Vi2_0012 Vi2_1021 Si2_1002 av Vi2_0031 q2_00 Vi2_1031 A00 q2_10 A01 A02 m00 A03 m01 m02 Si2_1102 Vi2_1122 m03 Si2_2002 q2_11 Vip002 Sip021 A10 Vi2_2101 A11 Si2_2021 Vi2_2031 Vi2_2111 A12 Si2_2122 q2_20 A13 m10 Si1_0101 q2_21 Si1_0001 m11 A20 m12 Sip031 A21 m13 Si1_0111 A22 m20 Si1_0011 A23 m21 Sip103 q1_00 A30 m22 A31 m23 A32 m30 Sip202 A33 m31 A40 m32 Sip131 A41 m33 Si1_0202 A42 q1_01 qp0 A43 Vip221 A50 Sip302 q1_02 A51 m40 A52 m41 Si1_1101 A53 Vip231 Si1_3101 qp1 Sip321 qp2 Si1_1111 m42 B00 Si1_1201 m43 m50 Si1_3202 m51 A60 m52 B01 Si1_3111 q1_11 Si1_2202 m53 A61 o00 A62 q1_31 Si1_3001 A63 Vi1_2101 q1_32 Sip501 A70 m60 A71 Si1_1211 o01 A72 Si1_1002 m61 A73 m62 A80 Si1_2001 m63 A81 q1_12 Si1_2111 q1_22 A82 q1_10 Sip511 m70 A83 Si1_2011 m71 B02 Si1_3011 m72 B03 Sip522 q1_21 q1_20 m73 B04 Sip401 m80 q1_30 B05 Sip331 qp5 Sip413 B06 m81 m82 B07 qp3 Sip601 m83 Sip701 qp4 o02 Sip801 B10 o03 Sip713 B11 o04 o05 B12 o06 Sip611 B13 o07 Sip813 o10 B14 o11 B15 o12 Sip622 qp7 B16 qp8 B17 qp6 o13 B20 o14 B21 o15 o16 B22 o17 B23 o20 o21 B24 o22 B25 o23 o24 B26 o25 B27 o26 o27"
+LOADS = "Lw2_10 Lw2_00 Lw2_01 Lw2_21 Lw2_11 Lw1_12 Lw2_20 Lg0 Lgs Lw1_02 Lw1_11 Lsb0 Lsa0 Lw1_10 Lg1 Lgs2 Lsa1 Lsb1 Lw1_01 Lsa4 Lsb4 Lsb3 Lsa3 Lsa2 Lsb2 Lsa5 Lg2 Lsb5 Lw1_00 Lsa8 Lsb8 Lsa7 Lsa6 Lsb6 Lsb7"
+ORDER = "Vi2_1004 Si2_0001 Vi2_0012 Vi2_0113 Si2_0101 av Vi2_0031 q2_00 Vi2_2101 q2_10 Si2_2112 Vi2_1103 Si2_1131 Vi1_1201 Si2_2131 q2_11 Si2_2002 Vi1_1211 q2_01 A121 Vi2_2022 Si1_1231 A022 Vi1_1221 A033 Si1_0202 Vi1_0222 A014 q2_20 A135 Si1_1104 q1_02 A006 q2_21 A117 Vm01 A100 q1_12 A224 Vm03 Si1_1002 gi1_10b<q2_11 Vm00 Vm02 q1_10b A323 Sip001 q1_10a A406 q1_11 Sm32 A312 Vm11 Sip013 A333 Vm12 A307 Vm10 gi1_01b<q2_01 A431 Vm13 Sm30 A420 Vm43 Sm31 A415 q1_01b Sm33 A237 Vm40 Si1_0101 A201 gbp3b<q1_01b Vm41 A212 Sip101 Vm42 A523 Si1_0111 Vm21 A536 Sip113 Vm22 A515 Vm20 A500 Vm23 A812 qp0 Sip201 A824 qp1 Sip401 A631 Vm50 gbp3a<qp0 A627 Sip213 Vm51 A830 Vm52 A805 Vm53 A603 Si1_0022 Vm80 A616 Vm82 A715 Sm61 qp2 A734 Sm62 q1_01a A726 Vm83 gi1_00a<qp2 Sm60 B057 Vm81 Sm63 Vm72 B070 Sip411 q1_00b Sip501 q1_00a A703 qp3b Sip421 qp3a B032 Vm73 gbp6a<qp3b Sip512 Vm71 B021 Vo03 B006 Sip431 Vm70 Sip531 Vo07 B064 Sip802 Vo05 B015 qp5 qp4 Sip701 B042 St05 Vo01 Sip821 St03 gbp6b<qp4 B143 Vo06 Sip713 St07 Vo00 B120 Vo02 St06 B107 Vo14 Sip831 St01 Vo04 B155 St00 Vo10 B134 St14 qp6b qp8 B166 St02 qp6a qp7 St10 B111 Vo12 St04 B243 Vo15 Vo16 B212 St12 Vo24 St15 B277 Vo13 St16 Vo21 B200 St24 Vo27 B175 St13 Vo11 St21 B266 Vo20 St27 B253 Vo26 St11 B234 Vo17 St20 Vo25 B222 St26 Vo23 St17 Vo22 St25 St23 St22"
 
 
 def pieces(n):
@@ -37,30 +38,32 @@ def tile_token_mixing_input_gradient_e3_kernel(tc, g_words, g_scales, w2, w1, sl
     nc = tc.nc
     with ExitStack() as ctx:
         keep = ctx.enter_context(tc.tile_pool(name="keep", bufs=1))
-        ring = ctx.enter_context(tc.tile_pool(name="ring", bufs=24))
-        psum = ctx.enter_context(tc.psum_pool(name="psum", bufs=8))
+        ring = ctx.enter_context(tc.tile_pool(name="ring", bufs=25))
+        wide = ctx.enter_context(tc.tile_pool(name="wide", bufs=2))
+        psum = ctx.enter_context(tc.psum_pool(name="psum", bufs=1))
         ctx.enter_context(tc.manual_schedule())
 
+        banks = [psum.tile([P, 512], F32, name="bank%d" % i) for i in range(8)]
+
+        cols = keep.tile([P, 16], F32)
+        nc.vector.memset(cols[:], 0.0)
         gs0 = keep.tile([P, 2, 512], U8, align_bytes=64)
         gs12 = keep.tile([P, 2, 1024], U8, align_bytes=64)
         nc.vector.memset(gs0[:].rearrange("p g n -> p (g n)").bitcast(I32), 0)
         nc.vector.memset(gs12[:].rearrange("p g n -> p (g n)").bitcast(I32), 0)
 
-        cols = keep.tile([P, 16], F32)
-        nc.gpsimd.memset(cols[:], 0.0)
         aw = alpha.bitcast(F32)
         vw = v.bitcast(F32)
         with nc.allow_non_contiguous_dma(reason="one word a partition"):
-            nc.gpsimd.dma_start(out=cols[:, 0:1], in_=aw[0:128].rearrange("(p o) -> p o", o=1))
-            nc.gpsimd.dma_start(out=cols[0:64, 8:9], in_=aw[128:192].rearrange("(p o) -> p o", o=1))
-            nc.gpsimd.dma_start(out=cols[64:66, 8:9], in_=vw.rearrange("(p o) -> p o", o=1))
+            nc.scalar.dma_start(out=cols[:, 0:1], in_=aw[0:128].rearrange("(p o) -> p o", o=1))
+            nc.scalar.dma_start(out=cols[0:64, 8:9], in_=aw[128:192].rearrange("(p o) -> p o", o=1))
+            nc.scalar.dma_start(out=cols[64:66, 8:9], in_=vw.rearrange("(p o) -> p o", o=1))
         ident = keep.tile([P, P], F32)
         make_identity(nc, ident[:])
-        spread = psum.tile([P, 512], F32, name="bank")
-        nc.tensor.transpose(spread[:, 0:128], cols[:, 0:1].to_broadcast([P, P]), ident[:])
-        nc.tensor.transpose(spread[:, 128:256], cols[:, 8:9].to_broadcast([P, P]), ident[:])
-        avw = keep.tile([P, 256], F32)
-        av16 = avw[:].bitcast(BF16)
+        nc.tensor.transpose(banks[0][:, 0:128], cols[:, 0:1].to_broadcast([P, P]), ident[:])
+        nc.tensor.transpose(banks[0][:, 128:256], cols[:, 8:9].to_broadcast([P, P]), ident[:])
+        vcol = keep.tile([P, B], F32)
+        av = keep.tile([P, NC], F32)
 
         gw = keep.tile([P, 3, 2, 512], U32, align_bytes=64)
         w2c = keep.tile([P, 2, D], U32, align_bytes=64)
@@ -70,13 +73,12 @@ def tile_token_mixing_input_gradient_e3_kernel(tc, g_words, g_scales, w2, w1, sl
         pc = keep.tile([P, 9, 512], U32, align_bytes=64)
         psc = keep.tile([P, 9, 512], U8, align_bytes=64)
         sl = keep.tile([P, 9, 4, 512], BF16)
-        w1a = keep.tile([P, 3, 4, 256], BF16)
-        w1b = keep.tile([P, 3, 4, 768], BF16)
         tiles = {}
+        order = ORDER.split()
 
-        def buf(key, shape, dtype):
+        def buf(key, shape, dtype, pool=ring):
             if key not in tiles:
-                fresh = ring.tile(shape, dtype, name="buf", align_bytes=64)
+                fresh = pool.tile(shape, dtype, name="buf", align_bytes=64)
                 tiles[key] = fresh
             return tiles[key]
 
@@ -86,10 +88,11 @@ def tile_token_mixing_input_gradient_e3_kernel(tc, g_words, g_scales, w2, w1, sl
                                   in_=g_scales[:, 4 * q:4 * q + 4, c0:c1].rearrange("g r n -> r g n").bitcast(I32))
 
         for tok in LOADS.split():
-            if tok.startswith("Lw2_"):
-                c, g = int(tok[4]), int(tok[5])
-                raw = buf(("raw", c, g), [P, 4, 512], BF16)
-                nc.sync.dma_start(out=raw[:], in_=w2[512 * g:512 * (g + 1), 512 * c:512 * (c + 1)].rearrange("(p j) w -> p j w", j=4))
+            if tok.startswith("Lw"):
+                a, g = int(tok[4]), int(tok[5])
+                raw = buf("raw" + tok[2:], [P, 4, 512], BF16)
+                src = w2 if tok[2] == "2" else w1
+                nc.sync.dma_start(out=raw[:], in_=src[512 * g:512 * (g + 1), 512 * a:512 * (a + 1)].rearrange("(p j) w -> p j w", j=4))
             elif tok == "Lgs":
                 scale_rows(gs0, 0, 512)
             elif tok == "Lgs2":
@@ -98,18 +101,12 @@ def tile_token_mixing_input_gradient_e3_kernel(tc, g_words, g_scales, w2, w1, sl
                 n = int(tok[2])
                 nc.sync.dma_start(out=gw[:, n].bitcast(I32),
                                   in_=g_words[:, :, 512 * n:512 * (n + 1), :].rearrange("g p n t -> p g (n t)").bitcast(I32))
-            elif tok.startswith("Ls"):
+            else:
                 k = int(tok[3])
                 n, c = divmod(k, 3)
                 b, c0, c1, off = pieces(n)[0 if tok[2] == "a" else 1]
                 nc.sync.dma_start(out=sl[:, k, :, off:off + c1 - c0],
                                   in_=slope[b, 512 * c:512 * (c + 1), c0:c1].rearrange("(p t) x -> p t x", t=4))
-            elif tok.startswith("Lw1a"):
-                c = int(tok[4])
-                nc.sync.dma_start(out=w1a[:, c], in_=w1[512 * c:512 * (c + 1), 0:256].rearrange("(p j) w -> p j w", j=4))
-            else:
-                c = int(tok[4])
-                nc.sync.dma_start(out=w1b[:, c], in_=w1[512 * c:512 * (c + 1), 256:S].rearrange("(p j) w -> p j w", j=4))
 
         def move(eng, dst, src):
             if eng == "V":
@@ -119,72 +116,105 @@ def tile_token_mixing_input_gradient_e3_kernel(tc, g_words, g_scales, w2, w1, sl
             else:
                 nc.gpsimd.tensor_scalar(out=dst, in0=src, scalar1=1.0, scalar2=0.0, op0=MULT, op1=ADD)
 
-        def interleave(eng, dst, src):
-            move(eng, dst.rearrange("p (x i j) -> p x j i", i=4, j=4), src.rearrange("p j (x i) -> p x j i", i=4))
+        def words(ap):
+            return ap.rearrange("p (x i j) -> p x j i", i=4, j=4)
 
-        def store(n, m0, cnt, res):
-            for (b, c0, c1, off) in pieces(n):
-                nc.sync.dma_start(out=out[b, 128 * m0:128 * (m0 + cnt), c0:c1].rearrange("(r p) x -> p r x", p=P),
-                                  in_=res[:, m0 % 2:m0 % 2 + cnt, off:off + c1 - c0])
+        def rows(ap):
+            return ap.rearrange("p j (x i) -> p x j i", i=4)
 
-        for tok in ORDER.split():
-            if tok == "av":
-                nc.scalar.copy(out=avw[:], in_=spread[:, 0:256])
-            elif tok[1:].startswith("i2_"):
-                c, g, u, cnt = int(tok[4]), int(tok[5]), int(tok[6]), int(tok[7])
-                grp = buf(("g2", c, g), [P, 2048], BF16)
-                src = tiles[("raw", c, g)][:].rearrange("p j (m i t) -> p t m j i", i=2, t=4)
+        def grouped(name, u, cnt):
+            if "q" + name in order:
+                return buf("g" + name, [P, 2048], BF16)[:, 512 * u:512 * (u + cnt)]
+            half = buf("g" + name + "ab"[u // 2], [P, 1024], BF16)
+            return half[:, 512 * (u % 2):512 * (u % 2 + cnt)]
+
+        def interleave(eng, name, u, cnt):
+            if name[0] == "2":
+                src = tiles["raw" + name][:].rearrange("p j (m i t) -> p t m j i", i=2, t=4)
                 for t in range(u, u + cnt):
-                    move(tok[0], grp[:, 512 * t:512 * (t + 1)].rearrange("p (m i j) -> p m j i", i=2, j=4), src[:, t])
-            elif tok[1:].startswith("i1_"):
-                h, c, u, cnt = int(tok[4]), int(tok[5]), int(tok[6]), int(tok[7])
-                grp = buf(("g1", h, c), [P, 1024], BF16)
-                src = w1a[:, c] if h == 0 else w1b[:, c, :, 256 * (h - 1):256 * h]
-                interleave(tok[0], grp[:, 512 * u:512 * (u + cnt)], src[:, :, 128 * u:128 * (u + cnt)])
-            elif tok[1:].startswith("ip"):
-                k, u, cnt = int(tok[3]), int(tok[4]), int(tok[5])
-                grp = buf(("gp", k), [P, 2048], BF16)
-                interleave(tok[0], grp[:, 512 * u:512 * (u + cnt)], sl[:, k, :, 128 * u:128 * (u + cnt)])
-            elif tok.startswith("q2_"):
-                c, g = int(tok[3]), int(tok[4])
-                nc.vector.quantize_mx(out=w2c[:, g, 512 * c:512 * (c + 1)].bitcast(E4), scales=w2s[:, g, 512 * c:512 * (c + 1)],
-                                      in_=tiles[("g2", c, g)][:])
-            elif tok.startswith("q1_"):
-                h, c = int(tok[3]), int(tok[4])
-                nc.vector.quantize_mx(out=w1c[:, c, 256 * h:256 * (h + 1)].bitcast(E4), scales=w1s[:, c, 256 * h:256 * (h + 1)],
-                                      in_=tiles[("g1", h, c)][:])
-            elif tok.startswith("qp"):
-                k = int(tok[2])
-                nc.vector.quantize_mx(out=pc[:, k, :].bitcast(E5), scales=psc[:, k, :], in_=tiles[("gp", k)][:])
+                    move(eng, grouped(name, t, 1).rearrange("p (m i j) -> p m j i", i=2, j=4), src[:, t])
+            else:
+                src = tiles["raw" + name][:] if name[0] == "1" else sl[:, int(name[1])]
+                move(eng, words(grouped(name, u, cnt)), rows(src[:, :, 128 * u:128 * (u + cnt)]))
+
+        flat_out = out.rearrange("b s c -> (b s c)")
+
+        for tok in order:
+            if tok == "av":
+                spread = banks[0][:, 0:256].bitcast(BF16)
+                nc.scalar.copy(out=vcol[:], in_=spread[:, C:C + B])
+                for b in range(B):
+                    nc.scalar.activation(out=av[:, b * C:(b + 1) * C], in_=spread[:, 0:C], func=COPY, scale=vcol[:, b:b + 1])
+            elif tok[1] == "i" and tok[0] != "g":
+                interleave(tok[0], tok[2:-2], int(tok[-2]), int(tok[-1]))
+            elif tok.startswith("go"):
+                res = tiles["res" + tok[2:4]]
+                n = int(tok[2])
+                nc.gpsimd.tensor_tensor(out=res[:], in0=res[:], in1=av[:, 512 * n:512 * (n + 1)], op=MULT)
+            elif tok[0] == "g":
+                parts = tok.split("<")
+                name, half = parts[0][2:-1], "ab".index(parts[0][-1])
+                if len(parts) == 2:
+                    tiles["g" + parts[0][2:]] = tiles["g" + parts[1][1:]][:, 0:1024]
+                if tok[1] == "i":
+                    interleave("G", name, 2 * half, 2)
+                else:
+                    k = int(name[1])
+                    xs = slice(256 * half, 256 * (half + 1))
+                    nc.gpsimd.tensor_tensor(out=words(grouped(name, 2 * half, 2)), in0=rows(tiles["h" + name[1]][:, :, xs]),
+                                            in1=rows(sl[:, k, :, xs]), op=MULT)
+            elif tok[0] == "q":
+                lo, hi = (0, 512) if tok[-1] not in "ab" else (256 * "ab".index(tok[-1]), 256 * ("ab".index(tok[-1]) + 1))
+                src = tiles["g" + tok[1:]][:]
+                if tok[1] == "p":
+                    k = int(tok[2])
+                    nc.vector.quantize_mx(out=pc[:, k, lo:hi].bitcast(E5), scales=psc[:, k, lo:hi], in_=src)
+                else:
+                    a, g = int(tok[3]), int(tok[4])
+                    codes, scales = (w2c, w2s) if tok[1] == "2" else (w1c, w1s)
+                    nc.vector.quantize_mx(out=codes[:, g, 512 * a + lo:512 * a + hi].bitcast(E4),
+                                          scales=scales[:, g, 512 * a + lo:512 * a + hi], in_=src)
             elif tok[0] == "A":
                 k, t = int(tok[1]), int(tok[2])
                 n, c = divmod(k, 3)
-                bank = psum.tile([P, 512], F32, name="bank")
-                tiles[tok[1:], "A"] = bank
+                bank = banks[int(tok[3])]
+                tiles[tok[:3]] = bank
                 mc = slice(512 * c + 128 * t, 512 * c + 128 * (t + 1))
                 for g in range(2):
                     gsc = gs0[:, g, :] if n == 0 else gs12[:, g, 512 * (n - 1):512 * n]
                     nc.tensor.matmul_mx(out=bank[:], lhsT=w2c[:, g, mc].bitcast(E4), lhsT_scale=w2s[:, g, mc],
                                         rhs=gw[:, n, g, :].bitcast(E5), rhs_scale=gsc, start=(g == 0), stop=(g == 1))
-            elif tok[0] == "m":
-                k, t = int(tok[1]), int(tok[2])
-                nc.vector.tensor_tensor(out=sl[:, k, t, :], in0=tiles[tok[1:], "A"][:], in1=sl[:, k, t, :], op=MULT)
             elif tok[0] == "B":
                 n, m = int(tok[1]), int(tok[2])
-                bank = psum.tile([P, 512], F32, name="bank")
-                tiles[tok[1:], "B"] = bank
+                bank = banks[int(tok[3])]
+                tiles[tok[:3]] = bank
                 mc = slice(128 * m, 128 * (m + 1))
                 for c in range(3):
                     nc.tensor.matmul_mx(out=bank[:], lhsT=w1c[:, c, mc].bitcast(E4), lhsT_scale=w1s[:, c, mc],
                                         rhs=pc[:, 3 * n + c, :].bitcast(E5), rhs_scale=psc[:, 3 * n + c, :], start=(c == 0), stop=(c == 2))
+            elif tok[1] == "m":
+                k, t = int(tok[2]), int(tok[3])
+                bank = tiles["A" + tok[2:]]
+                if tok[0] == "V":
+                    nc.vector.tensor_tensor(out=sl[:, k, t, :], in0=bank[:], in1=sl[:, k, t, :], op=MULT)
+                else:
+                    nc.scalar.copy(out=buf("h" + tok[2], [P, 4, 512], F32, wide)[:, t, :], in_=bank[:])
+            elif tok[1] == "o":
+                n = int(tok[2])
+                res = buf("res" + tok[2:], [P, 512], F32)
+                bank = tiles["B" + tok[2:]]
+                if tok[0] == "V":
+                    nc.vector.tensor_tensor(out=res[:], in0=bank[:], in1=av[:, 512 * n:512 * (n + 1)], op=MULT)
+                else:
+                    nc.scalar.copy(out=res[:], in_=bank[:])
             else:
-                n, m = int(tok[1]), int(tok[2])
-                res = buf(("res", n, m // 2), [P, 2, 512], F32)
-                bank = tiles[tok[1:], "B"]
-                for (b, c0, c1, off) in pieces(n):
-                    nc.vector.scalar_tensor_tensor(out=res[:, m % 2, off:off + c1 - c0], in0=bank[:, off:off + c1 - c0],
-                                                   scalar=av16[:, C + b:C + b + 1], in1=av16[:, c0:c1], op0=MULT, op1=MULT)
-                if n == 2 and m >= 6:
-                    store(n, m, 1, res)
-                elif m % 2 == 1:
-                    store(n, m - 1, 2, res)
+                n, m = int(tok[2]), int(tok[3])
+                res = tiles["res" + tok[2:]]
+                if n == 1:
+                    first = S * C + 128 * m * C + 128
+                    step = S * C - 128
+                    dst = flat_out[first:first + 2 * step].rearrange("(u r) -> u r", u=2)[:, 0:P * C].rearrange("u (p x) -> p u x", p=P)[:, :, 0:256]
+                    nc.sync.dma_start(out=dst, in_=res[:].rearrange("p (u x) -> p u x", u=2))
+                else:
+                    for (b, c0, c1, off) in pieces(n):
+                        nc.sync.dma_start(out=out[b, 128 * m:128 * (m + 1), c0:c1], in_=res[:, off:off + c1 - c0])

@@ -4,217 +4,364 @@ import concourse.mybir as mybir
 from concourse.masks import make_identity
 
 S, D, B, C = 1024, 1536, 4, 384
-NC = B * C
-FLOPS = 2 * 2 * S * D * NC
+COLS = B * C
+FLOPS = 2 * 2 * S * D * COLS
 
 F32 = mybir.dt.float32
 BF16 = mybir.dt.bfloat16
 U32 = mybir.dt.uint32
 I32 = mybir.dt.int32
 U8 = mybir.dt.uint8
-E4 = mybir.dt.float8_e4m3fn_x4
-E5 = mybir.dt.float8_e5m2_x4
+E4M3 = mybir.dt.float8_e4m3fn_x4
+E5M2 = mybir.dt.float8_e5m2_x4
 MULT = mybir.AluOpType.mult
 ADD = mybir.AluOpType.add
 COPY = mybir.ActivationFunctionType.Copy
+
 P = 128
+PACK = 4
+W = 512
+QUARTER = W // 4
+BANKS = 8
+RING_BUFS = 25
+H_BUFS = 2
+LAST_FIRST = (3, 2, 1, 0)
 
-LOADS = "Lw2_10 Lw2_00 Lw2_01 Lw2_21 Lw2_11 Lw1_12 Lw2_20 Lg0 Lgs Lw1_02 Lw1_11 Lsb0 Lsa0 Lw1_10 Lg1 Lgs2 Lsa1 Lsb1 Lw1_01 Lsa4 Lsb4 Lsb3 Lsa3 Lsa2 Lsb2 Lsa5 Lg2 Lsb5 Lw1_00 Lsa8 Lsb8 Lsa7 Lsa6 Lsb6 Lsb7"
-ORDER = "Vi2_1004 Si2_0001 Vi2_0012 Vi2_0113 Si2_0101 av Vi2_0031 q2_00 Vi2_2101 q2_10 Si2_2112 Vi2_1103 Si2_1131 Vi1_1201 Si2_2131 q2_11 Si2_2002 Vi1_1211 q2_01 A121 Vi2_2022 Si1_1231 A022 Vi1_1221 A033 Si1_0202 Vi1_0222 A014 q2_20 A135 Si1_1104 q1_02 A006 q2_21 A117 Vm01 A100 q1_12 A224 Vm03 Si1_1002 gi1_10b<q2_11 Vm00 Vm02 q1_10b A323 Sip001 q1_10a A406 q1_11 Sm32 A312 Vm11 Sip013 A333 Vm12 A307 Vm10 gi1_01b<q2_01 A431 Vm13 Sm30 A420 Vm43 Sm31 A415 q1_01b Sm33 A237 Vm40 Si1_0101 A201 gbp3b<q1_01b Vm41 A212 Sip101 Vm42 A523 Si1_0111 Vm21 A536 Sip113 Vm22 A515 Vm20 A500 Vm23 A812 qp0 Sip201 A824 qp1 Sip401 A631 Vm50 gbp3a<qp0 A627 Sip213 Vm51 A830 Vm52 A805 Vm53 A603 Si1_0022 Vm80 A616 Vm82 A715 Sm61 qp2 A734 Sm62 q1_01a A726 Vm83 gi1_00a<qp2 Sm60 B057 Vm81 Sm63 Vm72 B070 Sip411 q1_00b Sip501 q1_00a A703 qp3b Sip421 qp3a B032 Vm73 gbp6a<qp3b Sip512 Vm71 B021 Vo03 B006 Sip431 Vm70 Sip531 Vo07 B064 Sip802 Vo05 B015 qp5 qp4 Sip701 B042 St05 Vo01 Sip821 St03 gbp6b<qp4 B143 Vo06 Sip713 St07 Vo00 B120 Vo02 St06 B107 Vo14 Sip831 St01 Vo04 B155 St00 Vo10 B134 St14 qp6b qp8 B166 St02 qp6a qp7 St10 B111 Vo12 St04 B243 Vo15 Vo16 B212 St12 Vo24 St15 B277 Vo13 St16 Vo21 B200 St24 Vo27 B175 St13 Vo11 St21 B266 Vo20 St27 B253 Vo26 St11 B234 Vo17 St20 Vo25 B222 St26 Vo23 St17 Vo22 St25 St23 St22"
 
-
-def pieces(n):
-    res = []
-    col = 512 * n
-    while col < 512 * (n + 1):
-        b = col // C
-        end = min((b + 1) * C, 512 * (n + 1))
-        res.append((b, col - b * C, end - b * C, col - 512 * n))
-        col = end
-    return res
+def image_pieces(n):
+    first = W * n
+    image = first // C
+    split = (image + 1) * C
+    return [(image, first - image * C, C, 0), (image + 1, 0, first + W - split, split - first)]
 
 
 def tile_token_mixing_input_gradient_e3_kernel(tc, g_words, g_scales, w2, w1, slope, alpha, v, out):
     nc = tc.nc
     with ExitStack() as ctx:
         keep = ctx.enter_context(tc.tile_pool(name="keep", bufs=1))
-        ring = ctx.enter_context(tc.tile_pool(name="ring", bufs=25))
-        wide = ctx.enter_context(tc.tile_pool(name="wide", bufs=2))
+        ring = ctx.enter_context(tc.tile_pool(name="ring", bufs=RING_BUFS))
+        h_pool = ctx.enter_context(tc.tile_pool(name="h_pool", bufs=H_BUFS))
         psum = ctx.enter_context(tc.psum_pool(name="psum", bufs=1))
         ctx.enter_context(tc.manual_schedule())
 
-        banks = [psum.tile([P, 512], F32, name="bank%d" % i) for i in range(8)]
+        banks = [psum.tile([P, W], F32, name="bank%d" % i) for i in range(BANKS)]
+        free_banks = list(range(1, BANKS))
+        factor_bank = banks[0]
 
-        cols = keep.tile([P, 16], F32)
-        nc.vector.memset(cols[:], 0.0)
-        gs0 = keep.tile([P, 2, 512], U8, align_bytes=64)
-        gs12 = keep.tile([P, 2, 1024], U8, align_bytes=64)
-        nc.vector.memset(gs0[:].rearrange("p g n -> p (g n)").bitcast(I32), 0)
-        nc.vector.memset(gs12[:].rearrange("p g n -> p (g n)").bitcast(I32), 0)
+        def take_bank():
+            number = free_banks[0]
+            free_banks.remove(number)
+            return number
 
-        aw = alpha.bitcast(F32)
-        vw = v.bitcast(F32)
-        with nc.allow_non_contiguous_dma(reason="one word a partition"):
-            nc.scalar.dma_start(out=cols[:, 0:1], in_=aw[0:128].rearrange("(p o) -> p o", o=1))
-            nc.scalar.dma_start(out=cols[0:64, 8:9], in_=aw[128:192].rearrange("(p o) -> p o", o=1))
-            nc.scalar.dma_start(out=cols[64:66, 8:9], in_=vw.rearrange("(p o) -> p o", o=1))
-        ident = keep.tile([P, P], F32)
-        make_identity(nc, ident[:])
-        nc.tensor.transpose(banks[0][:, 0:128], cols[:, 0:1].to_broadcast([P, P]), ident[:])
-        nc.tensor.transpose(banks[0][:, 128:256], cols[:, 8:9].to_broadcast([P, P]), ident[:])
-        vcol = keep.tile([P, B], F32)
-        av = keep.tile([P, NC], F32)
+        word_cols = keep.tile([P, 16], F32)
+        nc.vector.memset(word_cols[:], 0.0)
+        g_scale_first = keep.tile([P, 2, W], U8, align_bytes=64)
+        g_scale_rest = keep.tile([P, 2, 2 * W], U8, align_bytes=64)
+        nc.vector.memset(g_scale_first[:].rearrange("p g n -> p (g n)").bitcast(I32), 0)
+        nc.vector.memset(g_scale_rest[:].rearrange("p g n -> p (g n)").bitcast(I32), 0)
 
-        gw = keep.tile([P, 3, 2, 512], U32, align_bytes=64)
-        w2c = keep.tile([P, 2, D], U32, align_bytes=64)
-        w2s = keep.tile([P, 2, D], U8, align_bytes=64)
-        w1c = keep.tile([P, 3, S], U32, align_bytes=64)
-        w1s = keep.tile([P, 3, S], U8, align_bytes=64)
-        pc = keep.tile([P, 9, 512], U32, align_bytes=64)
-        psc = keep.tile([P, 9, 512], U8, align_bytes=64)
-        sl = keep.tile([P, 9, 4, 512], BF16)
-        tiles = {}
-        order = ORDER.split()
+        alpha_words = alpha.bitcast(F32).rearrange("(p o) -> p o", o=1)
+        v_words = v.bitcast(F32).rearrange("(p o) -> p o", o=1)
+        with nc.allow_non_contiguous_dma(reason="one word to a partition"):
+            nc.scalar.dma_start(out=word_cols[:, 0:1], in_=alpha_words[0:128])
+            nc.scalar.dma_start(out=word_cols[0:64, 8:9], in_=alpha_words[128:192])
+            nc.scalar.dma_start(out=word_cols[64:66, 8:9], in_=v_words)
+        identity = keep.tile([P, P], F32)
+        make_identity(nc, identity[:])
+        nc.tensor.transpose(factor_bank[:, 0:P], word_cols[:, 0:1].to_broadcast([P, P]), identity[:])
+        nc.tensor.transpose(factor_bank[:, P:2 * P], word_cols[:, 8:9].to_broadcast([P, P]), identity[:])
+        v_cols = keep.tile([P, B], F32)
+        factor = keep.tile([P, COLS], F32)
 
-        def buf(key, shape, dtype, pool=ring):
-            if key not in tiles:
-                fresh = pool.tile(shape, dtype, name="buf", align_bytes=64)
-                tiles[key] = fresh
-            return tiles[key]
+        g_codes = keep.tile([P, 3, 2, W], U32, align_bytes=64)
+        w2_codes = keep.tile([P, 2, D], U32, align_bytes=64)
+        w2_scales = keep.tile([P, 2, D], U8, align_bytes=64)
+        w1_codes = keep.tile([P, 3, S], U32, align_bytes=64)
+        w1_scales = keep.tile([P, 3, S], U8, align_bytes=64)
+        p_codes = keep.tile([P, 9, W], U32, align_bytes=64)
+        p_scales = keep.tile([P, 9, W], U8, align_bytes=64)
+        slope_sb = keep.tile([P, 9, PACK, W], BF16)
 
-        def scale_rows(dst, c0, c1):
+        raw = {}
+        interleaved = {}
+        sums = {}
+        h_copies = {}
+        results = {}
+
+        def load_weight(name, column_block, row_pass):
+            rows = (w2 if name == "w2" else w1)[W * row_pass:W * (row_pass + 1), W * column_block:W * (column_block + 1)]
+            tile = ring.tile([P, PACK, W], BF16, name="buf", align_bytes=64)
+            raw[name, column_block, row_pass] = tile
+            nc.sync.dma_start(out=tile[:], in_=rows.rearrange("(p j) w -> p j w", j=PACK))
+
+        def load_g_scales(plane, first, end):
             for q in range(4):
-                nc.sync.dma_start(out=dst[32 * q:32 * q + 4].bitcast(I32),
-                                  in_=g_scales[:, 4 * q:4 * q + 4, c0:c1].rearrange("g r n -> r g n").bitcast(I32))
+                rows = g_scales[:, 4 * q:4 * q + 4, first:end].rearrange("g r n -> r g n")
+                nc.sync.dma_start(out=plane[32 * q:32 * q + 4].bitcast(I32), in_=rows.bitcast(I32))
 
-        for tok in LOADS.split():
-            if tok.startswith("Lw"):
-                a, g = int(tok[4]), int(tok[5])
-                raw = buf("raw" + tok[2:], [P, 4, 512], BF16)
-                src = w2 if tok[2] == "2" else w1
-                nc.sync.dma_start(out=raw[:], in_=src[512 * g:512 * (g + 1), 512 * a:512 * (a + 1)].rearrange("(p j) w -> p j w", j=4))
-            elif tok == "Lgs":
-                scale_rows(gs0, 0, 512)
-            elif tok == "Lgs2":
-                scale_rows(gs12, 512, NC)
-            elif tok.startswith("Lg"):
-                n = int(tok[2])
-                nc.sync.dma_start(out=gw[:, n].bitcast(I32),
-                                  in_=g_words[:, :, 512 * n:512 * (n + 1), :].rearrange("g p n t -> p g (n t)").bitcast(I32))
-            else:
-                k = int(tok[3])
-                n, c = divmod(k, 3)
-                b, c0, c1, off = pieces(n)[0 if tok[2] == "a" else 1]
-                nc.sync.dma_start(out=sl[:, k, :, off:off + c1 - c0],
-                                  in_=slope[b, 512 * c:512 * (c + 1), c0:c1].rearrange("(p t) x -> p t x", t=4))
+        def load_g(n):
+            words = g_words[:, :, W * n:W * (n + 1), :].rearrange("g p n t -> p g (n t)")
+            nc.sync.dma_start(out=g_codes[:, n].bitcast(I32), in_=words.bitcast(I32))
 
-        def move(eng, dst, src):
-            if eng == "V":
+        def load_slope(n, c, pieces=(0, 1)):
+            for piece in pieces:
+                image, first, end, column = image_pieces(n)[piece]
+                rows = slope[image, W * c:W * (c + 1), first:end].rearrange("(p t) x -> p t x", t=PACK)
+                nc.sync.dma_start(out=slope_sb[:, 3 * n + c, :, column:column + end - first], in_=rows)
+
+        for c in range(3):
+            for g in range(2):
+                load_weight("w2", c, g)
+        load_g_scales(g_scale_first, 0, W)
+        load_g(0)
+        load_weight("w1", 0, 0)
+        load_slope(0, 0)
+        load_weight("w1", 0, 1)
+        load_slope(0, 1)
+        load_slope(0, 2, (1,))
+        load_g_scales(g_scale_rest, W, COLS)
+        load_slope(0, 2, (0,))
+        load_g(2)
+        load_weight("w1", 0, 2)
+        load_slope(2, 1)
+        load_slope(2, 2, (1,))
+        load_weight("w1", 1, 0)
+        load_g(1)
+        load_slope(2, 2, (0,))
+        load_slope(1, 1, (0,))
+        load_slope(2, 0)
+        load_weight("w1", 1, 1)
+        load_slope(1, 1, (1,))
+        load_weight("w1", 1, 2)
+        load_slope(1, 2)
+        load_slope(1, 0)
+
+        def make_factor():
+            values = factor_bank[:, 0:2 * P].bitcast(BF16)
+            nc.scalar.copy(out=v_cols[:], in_=values[:, C:C + B])
+            for b in range(B):
+                nc.scalar.activation(out=factor[:, b * C:(b + 1) * C], in_=values[:, 0:C], func=COPY, scale=v_cols[:, b:b + 1])
+            free_banks.append(0)
+
+        def move(engine, dst, src):
+            if engine == "vector":
                 nc.vector.tensor_copy(out=dst, in_=src)
-            elif eng == "S":
+            elif engine == "scalar":
                 nc.scalar.copy(out=dst, in_=src)
             else:
                 nc.gpsimd.tensor_scalar(out=dst, in0=src, scalar1=1.0, scalar2=0.0, op0=MULT, op1=ADD)
 
-        def words(ap):
-            return ap.rearrange("p (x i j) -> p x j i", i=4, j=4)
+        def target(operand, half, after):
+            if after is not None:
+                interleaved[operand, half] = interleaved[after][:, 0:PACK * W // 2]
+            elif (operand, half) not in interleaved:
+                width = PACK * W if half is None else PACK * W // 2
+                tile = ring.tile([P, width], BF16, name="buf", align_bytes=64)
+                interleaved[operand, half] = tile
+            return interleaved[operand, half]
 
-        def rows(ap):
+        def as_words(ap):
+            return ap.rearrange("p (x i j) -> p x j i", i=4, j=PACK)
+
+        def as_rows(ap):
             return ap.rearrange("p j (x i) -> p x j i", i=4)
 
-        def grouped(name, u, cnt):
-            if "q" + name in order:
-                return buf("g" + name, [P, 2048], BF16)[:, 512 * u:512 * (u + cnt)]
-            half = buf("g" + name + "ab"[u // 2], [P, 1024], BF16)
-            return half[:, 512 * (u % 2):512 * (u % 2 + cnt)]
+        def interleave_w2(engine, c, g):
+            dst = target(("w2", c, g), None, None)
+            src = raw["w2", c, g][:].rearrange("p j (m i t) -> p t m j i", i=2, t=PACK)
+            for t in range(PACK):
+                move(engine, dst[:, W * t:W * (t + 1)].rearrange("p (m i j) -> p m j i", i=2, j=PACK), src[:, t])
 
-        def interleave(eng, name, u, cnt):
-            if name[0] == "2":
-                src = tiles["raw" + name][:].rearrange("p j (m i t) -> p t m j i", i=2, t=4)
-                for t in range(u, u + cnt):
-                    move(eng, grouped(name, t, 1).rearrange("p (m i j) -> p m j i", i=2, j=4), src[:, t])
+        def interleave(engine, operand, half=None, quarters=None, after=None):
+            name, a, c = operand
+            src = raw[operand][:] if name == "w1" else slope_sb[:, 3 * a + c]
+            dst = target(operand, half, after)
+            if half is not None:
+                move(engine, as_words(dst[:]), as_rows(src[:, :, W // 2 * half:W // 2 * (half + 1)]))
             else:
-                src = tiles["raw" + name][:] if name[0] == "1" else sl[:, int(name[1])]
-                move(eng, words(grouped(name, u, cnt)), rows(src[:, :, 128 * u:128 * (u + cnt)]))
+                first, end = quarters if quarters is not None else (0, 4)
+                move(engine, as_words(dst[:, W * first:W * end]), as_rows(src[:, :, QUARTER * first:QUARTER * end]))
 
-        flat_out = out.rearrange("b s c -> (b s c)")
+        def quantise(*parts):
+            for operand, half in parts:
+                name, a, b = operand
+                first, end = (0, W) if half is None else (W // 2 * half, W // 2 * (half + 1))
+                src = interleaved[operand, half][:]
+                if name == "p":
+                    nc.vector.quantize_mx(out=p_codes[:, 3 * a + b, first:end].bitcast(E5M2),
+                                          scales=p_scales[:, 3 * a + b, first:end], in_=src)
+                else:
+                    codes, scales = (w2_codes, w2_scales) if name == "w2" else (w1_codes, w1_scales)
+                    columns = slice(W * a + first, W * a + end)
+                    nc.vector.quantize_mx(out=codes[:, b, columns].bitcast(E4M3), scales=scales[:, b, columns], in_=src)
 
-        for tok in order:
-            if tok == "av":
-                spread = banks[0][:, 0:256].bitcast(BF16)
-                nc.scalar.copy(out=vcol[:], in_=spread[:, C:C + B])
-                for b in range(B):
-                    nc.scalar.activation(out=av[:, b * C:(b + 1) * C], in_=spread[:, 0:C], func=COPY, scale=vcol[:, b:b + 1])
-            elif tok[1] == "i" and tok[0] != "g":
-                interleave(tok[0], tok[2:-2], int(tok[-2]), int(tok[-1]))
-            elif tok.startswith("go"):
-                res = tiles["res" + tok[2:4]]
-                n = int(tok[2])
-                nc.gpsimd.tensor_tensor(out=res[:], in0=res[:], in1=av[:, 512 * n:512 * (n + 1)], op=MULT)
-            elif tok[0] == "g":
-                parts = tok.split("<")
-                name, half = parts[0][2:-1], "ab".index(parts[0][-1])
-                if len(parts) == 2:
-                    tiles["g" + parts[0][2:]] = tiles["g" + parts[1][1:]][:, 0:1024]
-                if tok[1] == "i":
-                    interleave("G", name, 2 * half, 2)
-                else:
-                    k = int(name[1])
-                    xs = slice(256 * half, 256 * (half + 1))
-                    nc.gpsimd.tensor_tensor(out=words(grouped(name, 2 * half, 2)), in0=rows(tiles["h" + name[1]][:, :, xs]),
-                                            in1=rows(sl[:, k, :, xs]), op=MULT)
-            elif tok[0] == "q":
-                lo, hi = (0, 512) if tok[-1] not in "ab" else (256 * "ab".index(tok[-1]), 256 * ("ab".index(tok[-1]) + 1))
-                src = tiles["g" + tok[1:]][:]
-                if tok[1] == "p":
-                    k = int(tok[2])
-                    nc.vector.quantize_mx(out=pc[:, k, lo:hi].bitcast(E5), scales=psc[:, k, lo:hi], in_=src)
-                else:
-                    a, g = int(tok[3]), int(tok[4])
-                    codes, scales = (w2c, w2s) if tok[1] == "2" else (w1c, w1s)
-                    nc.vector.quantize_mx(out=codes[:, g, 512 * a + lo:512 * a + hi].bitcast(E4),
-                                          scales=scales[:, g, 512 * a + lo:512 * a + hi], in_=src)
-            elif tok[0] == "A":
-                k, t = int(tok[1]), int(tok[2])
-                n, c = divmod(k, 3)
-                bank = banks[int(tok[3])]
-                tiles[tok[:3]] = bank
-                mc = slice(512 * c + 128 * t, 512 * c + 128 * (t + 1))
+        def stage1(n, c):
+            for t in range(PACK):
+                sums[1, n, PACK * c + t] = take_bank()
+                bank = banks[sums[1, n, PACK * c + t]]
+                columns = slice(W * c + P * t, W * c + P * (t + 1))
                 for g in range(2):
-                    gsc = gs0[:, g, :] if n == 0 else gs12[:, g, 512 * (n - 1):512 * n]
-                    nc.tensor.matmul_mx(out=bank[:], lhsT=w2c[:, g, mc].bitcast(E4), lhsT_scale=w2s[:, g, mc],
-                                        rhs=gw[:, n, g, :].bitcast(E5), rhs_scale=gsc, start=(g == 0), stop=(g == 1))
-            elif tok[0] == "B":
-                n, m = int(tok[1]), int(tok[2])
-                bank = banks[int(tok[3])]
-                tiles[tok[:3]] = bank
-                mc = slice(128 * m, 128 * (m + 1))
-                for c in range(3):
-                    nc.tensor.matmul_mx(out=bank[:], lhsT=w1c[:, c, mc].bitcast(E4), lhsT_scale=w1s[:, c, mc],
-                                        rhs=pc[:, 3 * n + c, :].bitcast(E5), rhs_scale=psc[:, 3 * n + c, :], start=(c == 0), stop=(c == 2))
-            elif tok[1] == "m":
-                k, t = int(tok[2]), int(tok[3])
-                bank = tiles["A" + tok[2:]]
-                if tok[0] == "V":
-                    nc.vector.tensor_tensor(out=sl[:, k, t, :], in0=bank[:], in1=sl[:, k, t, :], op=MULT)
-                else:
-                    nc.scalar.copy(out=buf("h" + tok[2], [P, 4, 512], F32, wide)[:, t, :], in_=bank[:])
-            elif tok[1] == "o":
-                n = int(tok[2])
-                res = buf("res" + tok[2:], [P, 512], F32)
-                bank = tiles["B" + tok[2:]]
-                if tok[0] == "V":
-                    nc.vector.tensor_tensor(out=res[:], in0=bank[:], in1=av[:, 512 * n:512 * (n + 1)], op=MULT)
-                else:
-                    nc.scalar.copy(out=res[:], in_=bank[:])
+                    g_scale = g_scale_first[:, g, :] if n == 0 else g_scale_rest[:, g, W * (n - 1):W * n]
+                    nc.tensor.matmul_mx(out=bank[:], lhsT=w2_codes[:, g, columns].bitcast(E4M3), lhsT_scale=w2_scales[:, g, columns],
+                                        rhs=g_codes[:, n, g, :].bitcast(E5M2), rhs_scale=g_scale, start=(g == 0), stop=(g == 1))
+
+        def times_slope(n, c, order=LAST_FIRST):
+            for t in order:
+                number = sums[1, n, PACK * c + t]
+                rows = slope_sb[:, 3 * n + c, t, :]
+                nc.vector.tensor_tensor(out=rows, in0=banks[number][:], in1=rows, op=MULT)
+                free_banks.append(number)
+
+        def copy_h(n, c):
+            tile = h_pool.tile([P, PACK, W], F32, name="h", align_bytes=64)
+            h_copies[n, c] = tile
+            for t in LAST_FIRST:
+                number = sums[1, n, PACK * c + t]
+                nc.scalar.copy(out=tile[:, t, :], in_=banks[number][:])
+                free_banks.append(number)
+
+        def times_slope_gpsimd(n, c, half, after=None):
+            columns = slice(W // 2 * half, W // 2 * (half + 1))
+            nc.gpsimd.tensor_tensor(out=as_words(target(("p", n, c), half, after)[:]), in0=as_rows(h_copies[n, c][:, :, columns]),
+                                    in1=as_rows(slope_sb[:, 3 * n + c, :, columns]), op=MULT)
+
+        def stage2_passes(n, m, passes):
+            if passes[0] == 0:
+                sums[2, n, m] = take_bank()
+            tokens = slice(P * m, P * (m + 1))
+            for c in passes:
+                nc.tensor.matmul_mx(out=banks[sums[2, n, m]][:], lhsT=w1_codes[:, c, tokens].bitcast(E4M3), lhsT_scale=w1_scales[:, c, tokens],
+                                    rhs=p_codes[:, 3 * n + c, :].bitcast(E5M2), rhs_scale=p_scales[:, 3 * n + c, :],
+                                    start=(c == 0), stop=(c == 2))
+
+        def stage2(n, h, last_pass_later=False):
+            tiles = range(4 * h, 4 * h + 4)
+            if last_pass_later:
+                for m in tiles:
+                    stage2_passes(n, m, (0, 1))
+                for m in tiles:
+                    stage2_passes(n, m, (2,))
             else:
-                n, m = int(tok[2]), int(tok[3])
-                res = tiles["res" + tok[2:]]
-                if n == 1:
-                    first = S * C + 128 * m * C + 128
-                    step = S * C - 128
-                    dst = flat_out[first:first + 2 * step].rearrange("(u r) -> u r", u=2)[:, 0:P * C].rearrange("u (p x) -> p u x", p=P)[:, :, 0:256]
-                    nc.sync.dma_start(out=dst, in_=res[:].rearrange("p (u x) -> p u x", u=2))
-                else:
-                    for (b, c0, c1, off) in pieces(n):
-                        nc.sync.dma_start(out=out[b, 128 * m:128 * (m + 1), c0:c1], in_=res[:, off:off + c1 - c0])
+                for m in tiles:
+                    stage2_passes(n, m, (0, 1, 2))
+
+        def result(n, m):
+            if (n, m // 2) not in results:
+                tile = ring.tile([P, 2, W], F32, name="buf", align_bytes=64)
+                results[n, m // 2] = tile
+            return results[n, m // 2][:, m % 2, :]
+
+        def times_factor(n, tiles):
+            for m in tiles:
+                nc.vector.tensor_tensor(out=result(n, m), in0=banks[sums[2, n, m]][:], in1=factor[:, W * n:W * (n + 1)], op=MULT)
+                free_banks.append(sums[2, n, m])
+
+        def times_factor_gpsimd(n, m):
+            nc.scalar.copy(out=result(n, m), in_=banks[sums[2, n, m]][:])
+            free_banks.append(sums[2, n, m])
+            nc.gpsimd.tensor_tensor(out=result(n, m), in0=result(n, m), in1=factor[:, W * n:W * (n + 1)], op=MULT)
+
+        def store_pair(n, m):
+            for image, first, end, column in image_pieces(n):
+                dst = out[image, P * m:P * (m + 2), first:end].rearrange("(r p) x -> p r x", p=P)
+                nc.sync.dma_start(out=dst, in_=results[n, m // 2][:, :, column:column + end - first])
+
+        def store_middle(m):
+            start = S * C + P * m * C + (C - W // 2)
+            step = S * C - (C - W // 2)
+            both = out.rearrange("b s c -> (b s c)")[start:start + 2 * step].rearrange("(u r) -> u r", u=2)
+            dst = both[:, 0:P * C].rearrange("u (p x) -> p u x", p=P)[:, :, 0:W // 2]
+            nc.sync.dma_start(out=dst, in_=result(1, m).rearrange("p (u x) -> p u x", u=2))
+
+        def finish_in_parts(n, m):
+            for image, first, end, column in image_pieces(n):
+                columns = slice(column, column + end - first)
+                nc.vector.tensor_tensor(out=result(n, m)[:, columns], in0=banks[sums[2, n, m]][:, columns],
+                                        in1=factor[:, W * n + column:W * n + column + end - first], op=MULT)
+                nc.sync.dma_start(out=out[image, P * m:P * (m + 1), first:end], in_=result(n, m)[:, columns])
+
+
+        interleave_w2("vector", 0, 0)
+        make_factor()
+        interleave_w2("vector", 0, 1)
+        interleave_w2("scalar", 1, 0)
+        quantise((("w2", 0, 0), None), (("w2", 0, 1), None))
+        interleave_w2("vector", 1, 1)
+        interleave_w2("scalar", 2, 0)
+        interleave_w2("vector", 2, 1)
+        quantise((("w2", 1, 0), None), (("w2", 1, 1), None), (("w2", 2, 0), None), (("w2", 2, 1), None))
+
+        stage1(0, 0)
+        interleave("scalar", ("w1", 0, 0))
+        stage1(0, 1)
+        times_slope(0, 0, (2, 1, 0, 3))
+        interleave("gpsimd", ("w1", 0, 1), half=0, after=(("w2", 2, 1), None))
+        stage1(0, 2)
+        times_slope(0, 1, (2, 1, 0, 3))
+        interleave("scalar", ("p", 0, 0))
+        interleave("gpsimd", ("w1", 0, 1), half=1)
+        times_slope(0, 2)
+        interleave("gpsimd", ("p", 0, 1), half=0)
+        interleave("scalar", ("p", 0, 1), half=1)
+        stage1(2, 1)
+        interleave("scalar", ("w1", 0, 2))
+        quantise((("p", 0, 1), 1), (("w1", 0, 0), None), (("p", 0, 0), None))
+        stage1(2, 0)
+        times_slope(2, 1)
+        interleave("gpsimd", ("p", 0, 2), half=1, after=(("w1", 0, 0), None))
+        interleave("scalar", ("p", 0, 2), half=0)
+        stage1(2, 2)
+        interleave("vector", ("w1", 1, 0), quarters=(0, 3))
+        copy_h(2, 0)
+        quantise((("p", 0, 2), 1), (("p", 0, 1), 0), (("p", 0, 2), 0),
+                 (("w1", 0, 1), 0), (("w1", 0, 1), 1), (("w1", 0, 2), None))
+
+        stage1(1, 1)
+        interleave("scalar", ("p", 2, 1))
+        times_slope(2, 2)
+        times_slope_gpsimd(2, 0, 0, after=(("w1", 0, 1), 1))
+        stage2(0, 0)
+        interleave("scalar", ("w1", 1, 0), quarters=(3, 4))
+        interleave("scalar", ("w1", 1, 1))
+        times_slope(1, 1)
+        times_slope_gpsimd(2, 0, 1)
+        stage1(1, 0)
+        times_factor(0, LAST_FIRST)
+        interleave("scalar", ("w1", 1, 2))
+        stage1(1, 2)
+        quantise((("w1", 1, 1), None), (("w1", 1, 0), None), (("p", 2, 0), 0),
+                 (("p", 2, 1), None), (("p", 2, 0), 1), (("w1", 1, 2), None))
+        copy_h(1, 0)
+        store_pair(0, 0)
+        store_pair(0, 2)
+        stage2(0, 1, last_pass_later=True)
+        interleave("scalar", ("p", 2, 2))
+        times_slope(1, 2)
+        times_slope_gpsimd(1, 0, 0, after=(("p", 2, 0), 1))
+        interleave("scalar", ("p", 1, 1))
+
+        times_factor(0, (5, 4))
+        quantise((("p", 2, 2), None), (("p", 1, 0), 0))
+        stage2(2, 0, last_pass_later=True)
+        store_pair(0, 4)
+        times_factor(0, (7, 6))
+        times_slope_gpsimd(1, 0, 1, after=(("p", 2, 2), None))
+        interleave("scalar", ("p", 1, 2))
+        times_factor(2, (1, 0))
+        stage2(2, 1)
+        store_pair(0, 6)
+        times_factor(2, (3, 2))
+        store_pair(2, 0)
+        quantise((("p", 1, 1), None), (("p", 1, 0), 1))
+        times_factor_gpsimd(2, 6)
+        times_factor(2, (5, 4, 7))
+        store_pair(2, 2)
+        quantise((("p", 1, 2), None))
+        stage2(1, 0, last_pass_later=True)
+        store_pair(2, 4)
+        store_pair(2, 6)
+        stage2(1, 1)
+        for m in range(7):
+            times_factor(1, (m,))
+            store_middle(m)
+        finish_in_parts(1, 7)

from contextlib import ExitStack

import concourse.mybir as mybir
from concourse.masks import make_identity

S, D, B, C = 1024, 1536, 4, 384
COLS = B * C
FLOPS = 2 * 2 * S * D * COLS

F32 = mybir.dt.float32
BF16 = mybir.dt.bfloat16
U32 = mybir.dt.uint32
I32 = mybir.dt.int32
U8 = mybir.dt.uint8
E4M3 = mybir.dt.float8_e4m3fn_x4
E5M2 = mybir.dt.float8_e5m2_x4
MULT = mybir.AluOpType.mult
ADD = mybir.AluOpType.add
COPY = mybir.ActivationFunctionType.Copy

P = 128
PACK = 4
W = 512
QUARTER = W // 4
BANKS = 8
RING_BUFS = 25
H_BUFS = 2
LAST_FIRST = (3, 2, 1, 0)


def image_pieces(n):
    first = W * n
    image = first // C
    split = (image + 1) * C
    return [(image, first - image * C, C, 0), (image + 1, 0, first + W - split, split - first)]


def tile_token_mixing_input_gradient_e3_kernel(tc, g_words, g_scales, w2, w1, slope, alpha, v, out):
    nc = tc.nc
    with ExitStack() as ctx:
        keep = ctx.enter_context(tc.tile_pool(name="keep", bufs=1))
        ring = ctx.enter_context(tc.tile_pool(name="ring", bufs=RING_BUFS))
        h_pool = ctx.enter_context(tc.tile_pool(name="h_pool", bufs=H_BUFS))
        psum = ctx.enter_context(tc.psum_pool(name="psum", bufs=1))
        ctx.enter_context(tc.manual_schedule())

        banks = [psum.tile([P, W], F32, name="bank%d" % i) for i in range(BANKS)]
        free_banks = list(range(1, BANKS))
        factor_bank = banks[0]

        def take_bank():
            number = free_banks[0]
            free_banks.remove(number)
            return number

        word_cols = keep.tile([P, 16], F32)
        nc.vector.memset(word_cols[:], 0.0)
        g_scale_first = keep.tile([P, 2, W], U8, align_bytes=64)
        g_scale_rest = keep.tile([P, 2, 2 * W], U8, align_bytes=64)
        nc.vector.memset(g_scale_first[:].rearrange("p g n -> p (g n)").bitcast(I32), 0)
        nc.vector.memset(g_scale_rest[:].rearrange("p g n -> p (g n)").bitcast(I32), 0)

        alpha_words = alpha.bitcast(F32).rearrange("(p o) -> p o", o=1)
        v_words = v.bitcast(F32).rearrange("(p o) -> p o", o=1)
        with nc.allow_non_contiguous_dma(reason="one word to a partition"):
            nc.scalar.dma_start(out=word_cols[:, 0:1], in_=alpha_words[0:128])
            nc.scalar.dma_start(out=word_cols[0:64, 8:9], in_=alpha_words[128:192])
            nc.scalar.dma_start(out=word_cols[64:66, 8:9], in_=v_words)
        identity = keep.tile([P, P], F32)
        make_identity(nc, identity[:])
        nc.tensor.transpose(factor_bank[:, 0:P], word_cols[:, 0:1].to_broadcast([P, P]), identity[:])
        nc.tensor.transpose(factor_bank[:, P:2 * P], word_cols[:, 8:9].to_broadcast([P, P]), identity[:])
        v_cols = keep.tile([P, B], F32)
        factor = keep.tile([P, COLS], F32)

        g_codes = keep.tile([P, 3, 2, W], U32, align_bytes=64)
        w2_codes = keep.tile([P, 2, D], U32, align_bytes=64)
        w2_scales = keep.tile([P, 2, D], U8, align_bytes=64)
        w1_codes = keep.tile([P, 3, S], U32, align_bytes=64)
        w1_scales = keep.tile([P, 3, S], U8, align_bytes=64)
        p_codes = keep.tile([P, 9, W], U32, align_bytes=64)
        p_scales = keep.tile([P, 9, W], U8, align_bytes=64)
        slope_sb = keep.tile([P, 9, PACK, W], BF16)

        raw = {}
        interleaved = {}
        sums = {}
        h_copies = {}
        results = {}

        def load_weight(name, column_block, row_pass):
            rows = (w2 if name == "w2" else w1)[W * row_pass:W * (row_pass + 1), W * column_block:W * (column_block + 1)]
            tile = ring.tile([P, PACK, W], BF16, name="buf", align_bytes=64)
            raw[name, column_block, row_pass] = tile
            nc.sync.dma_start(out=tile[:], in_=rows.rearrange("(p j) w -> p j w", j=PACK))

        def load_g_scales(plane, first, end):
            for q in range(4):
                rows = g_scales[:, 4 * q:4 * q + 4, first:end].rearrange("g r n -> r g n")
                nc.sync.dma_start(out=plane[32 * q:32 * q + 4].bitcast(I32), in_=rows.bitcast(I32))

        def load_g(n):
            words = g_words[:, :, W * n:W * (n + 1), :].rearrange("g p n t -> p g (n t)")
            nc.sync.dma_start(out=g_codes[:, n].bitcast(I32), in_=words.bitcast(I32))

        def load_slope(n, c, pieces=(0, 1)):
            for piece in pieces:
                image, first, end, column = image_pieces(n)[piece]
                rows = slope[image, W * c:W * (c + 1), first:end].rearrange("(p t) x -> p t x", t=PACK)
                nc.sync.dma_start(out=slope_sb[:, 3 * n + c, :, column:column + end - first], in_=rows)

        for c in range(3):
            for g in range(2):
                load_weight("w2", c, g)
        load_g_scales(g_scale_first, 0, W)
        load_g(0)
        load_weight("w1", 0, 0)
        load_slope(0, 0)
        load_weight("w1", 0, 1)
        load_slope(0, 1)
        load_slope(0, 2, (1,))
        load_g_scales(g_scale_rest, W, COLS)
        load_slope(0, 2, (0,))
        load_g(2)
        load_weight("w1", 0, 2)
        load_slope(2, 1)
        load_slope(2, 2, (1,))
        load_weight("w1", 1, 0)
        load_g(1)
        load_slope(2, 2, (0,))
        load_slope(1, 1, (0,))
        load_slope(2, 0)
        load_weight("w1", 1, 1)
        load_slope(1, 1, (1,))
        load_weight("w1", 1, 2)
        load_slope(1, 2)
        load_slope(1, 0)

        def make_factor():
            values = factor_bank[:, 0:2 * P].bitcast(BF16)
            nc.scalar.copy(out=v_cols[:], in_=values[:, C:C + B])
            for b in range(B):
                nc.scalar.activation(out=factor[:, b * C:(b + 1) * C], in_=values[:, 0:C], func=COPY, scale=v_cols[:, b:b + 1])
            free_banks.append(0)

        def move(engine, dst, src):
            if engine == "vector":
                nc.vector.tensor_copy(out=dst, in_=src)
            elif engine == "scalar":
                nc.scalar.copy(out=dst, in_=src)
            else:
                nc.gpsimd.tensor_scalar(out=dst, in0=src, scalar1=1.0, scalar2=0.0, op0=MULT, op1=ADD)

        def target(operand, half, after):
            if after is not None:
                interleaved[operand, half] = interleaved[after][:, 0:PACK * W // 2]
            elif (operand, half) not in interleaved:
                width = PACK * W if half is None else PACK * W // 2
                tile = ring.tile([P, width], BF16, name="buf", align_bytes=64)
                interleaved[operand, half] = tile
            return interleaved[operand, half]

        def as_words(ap):
            return ap.rearrange("p (x i j) -> p x j i", i=4, j=PACK)

        def as_rows(ap):
            return ap.rearrange("p j (x i) -> p x j i", i=4)

        def interleave_w2(engine, c, g):
            dst = target(("w2", c, g), None, None)
            src = raw["w2", c, g][:].rearrange("p j (m i t) -> p t m j i", i=2, t=PACK)
            for t in range(PACK):
                move(engine, dst[:, W * t:W * (t + 1)].rearrange("p (m i j) -> p m j i", i=2, j=PACK), src[:, t])

        def interleave(engine, operand, half=None, quarters=None, after=None):
            name, a, c = operand
            src = raw[operand][:] if name == "w1" else slope_sb[:, 3 * a + c]
            dst = target(operand, half, after)
            if half is not None:
                move(engine, as_words(dst[:]), as_rows(src[:, :, W // 2 * half:W // 2 * (half + 1)]))
            else:
                first, end = quarters if quarters is not None else (0, 4)
                move(engine, as_words(dst[:, W * first:W * end]), as_rows(src[:, :, QUARTER * first:QUARTER * end]))

        def quantise(*parts):
            for operand, half in parts:
                name, a, b = operand
                first, end = (0, W) if half is None else (W // 2 * half, W // 2 * (half + 1))
                src = interleaved[operand, half][:]
                if name == "p":
                    nc.vector.quantize_mx(out=p_codes[:, 3 * a + b, first:end].bitcast(E5M2),
                                          scales=p_scales[:, 3 * a + b, first:end], in_=src)
                else:
                    codes, scales = (w2_codes, w2_scales) if name == "w2" else (w1_codes, w1_scales)
                    columns = slice(W * a + first, W * a + end)
                    nc.vector.quantize_mx(out=codes[:, b, columns].bitcast(E4M3), scales=scales[:, b, columns], in_=src)

        def stage1(n, c):
            for t in range(PACK):
                sums[1, n, PACK * c + t] = take_bank()
                bank = banks[sums[1, n, PACK * c + t]]
                columns = slice(W * c + P * t, W * c + P * (t + 1))
                for g in range(2):
                    g_scale = g_scale_first[:, g, :] if n == 0 else g_scale_rest[:, g, W * (n - 1):W * n]
                    nc.tensor.matmul_mx(out=bank[:], lhsT=w2_codes[:, g, columns].bitcast(E4M3), lhsT_scale=w2_scales[:, g, columns],
                                        rhs=g_codes[:, n, g, :].bitcast(E5M2), rhs_scale=g_scale, start=(g == 0), stop=(g == 1))

        def times_slope(n, c, order=LAST_FIRST):
            for t in order:
                number = sums[1, n, PACK * c + t]
                rows = slope_sb[:, 3 * n + c, t, :]
                nc.vector.tensor_tensor(out=rows, in0=banks[number][:], in1=rows, op=MULT)
                free_banks.append(number)

        def copy_h(n, c):
            tile = h_pool.tile([P, PACK, W], F32, name="h", align_bytes=64)
            h_copies[n, c] = tile
            for t in LAST_FIRST:
                number = sums[1, n, PACK * c + t]
                nc.scalar.copy(out=tile[:, t, :], in_=banks[number][:])
                free_banks.append(number)

        def times_slope_gpsimd(n, c, half, after=None):
            columns = slice(W // 2 * half, W // 2 * (half + 1))
            nc.gpsimd.tensor_tensor(out=as_words(target(("p", n, c), half, after)[:]), in0=as_rows(h_copies[n, c][:, :, columns]),
                                    in1=as_rows(slope_sb[:, 3 * n + c, :, columns]), op=MULT)

        def stage2_passes(n, m, passes):
            if passes[0] == 0:
                sums[2, n, m] = take_bank()
            tokens = slice(P * m, P * (m + 1))
            for c in passes:
                nc.tensor.matmul_mx(out=banks[sums[2, n, m]][:], lhsT=w1_codes[:, c, tokens].bitcast(E4M3), lhsT_scale=w1_scales[:, c, tokens],
                                    rhs=p_codes[:, 3 * n + c, :].bitcast(E5M2), rhs_scale=p_scales[:, 3 * n + c, :],
                                    start=(c == 0), stop=(c == 2))

        def stage2(n, h, last_pass_later=False):
            tiles = range(4 * h, 4 * h + 4)
            if last_pass_later:
                for m in tiles:
                    stage2_passes(n, m, (0, 1))
                for m in tiles:
                    stage2_passes(n, m, (2,))
            else:
                for m in tiles:
                    stage2_passes(n, m, (0, 1, 2))

        def result(n, m):
            if (n, m // 2) not in results:
                tile = ring.tile([P, 2, W], F32, name="buf", align_bytes=64)
                results[n, m // 2] = tile
            return results[n, m // 2][:, m % 2, :]

        def times_factor(n, tiles):
            for m in tiles:
                nc.vector.tensor_tensor(out=result(n, m), in0=banks[sums[2, n, m]][:], in1=factor[:, W * n:W * (n + 1)], op=MULT)
                free_banks.append(sums[2, n, m])

        def times_factor_gpsimd(n, m):
            nc.scalar.copy(out=result(n, m), in_=banks[sums[2, n, m]][:])
            free_banks.append(sums[2, n, m])
            nc.gpsimd.tensor_tensor(out=result(n, m), in0=result(n, m), in1=factor[:, W * n:W * (n + 1)], op=MULT)

        def store_pair(n, m):
            for image, first, end, column in image_pieces(n):
                dst = out[image, P * m:P * (m + 2), first:end].rearrange("(r p) x -> p r x", p=P)
                nc.sync.dma_start(out=dst, in_=results[n, m // 2][:, :, column:column + end - first])

        def store_middle(m):
            start = S * C + P * m * C + (C - W // 2)
            step = S * C - (C - W // 2)
            both = out.rearrange("b s c -> (b s c)")[start:start + 2 * step].rearrange("(u r) -> u r", u=2)
            dst = both[:, 0:P * C].rearrange("u (p x) -> p u x", p=P)[:, :, 0:W // 2]
            nc.sync.dma_start(out=dst, in_=result(1, m).rearrange("p (u x) -> p u x", u=2))

        def finish_in_parts(n, m):
            for image, first, end, column in image_pieces(n):
                columns = slice(column, column + end - first)
                nc.vector.tensor_tensor(out=result(n, m)[:, columns], in0=banks[sums[2, n, m]][:, columns],
                                        in1=factor[:, W * n + column:W * n + column + end - first], op=MULT)
                nc.sync.dma_start(out=out[image, P * m:P * (m + 1), first:end], in_=result(n, m)[:, columns])


        interleave_w2("vector", 0, 0)
        make_factor()
        interleave_w2("vector", 0, 1)
        interleave_w2("scalar", 1, 0)
        quantise((("w2", 0, 0), None), (("w2", 0, 1), None))
        interleave_w2("vector", 1, 1)
        interleave_w2("scalar", 2, 0)
        interleave_w2("vector", 2, 1)
        quantise((("w2", 1, 0), None), (("w2", 1, 1), None), (("w2", 2, 0), None), (("w2", 2, 1), None))

        stage1(0, 0)
        interleave("scalar", ("w1", 0, 0))
        stage1(0, 1)
        times_slope(0, 0, (2, 1, 0, 3))
        interleave("gpsimd", ("w1", 0, 1), half=0, after=(("w2", 2, 1), None))
        stage1(0, 2)
        times_slope(0, 1, (2, 1, 0, 3))
        interleave("scalar", ("p", 0, 0))
        interleave("gpsimd", ("w1", 0, 1), half=1)
        times_slope(0, 2)
        interleave("gpsimd", ("p", 0, 1), half=0)
        interleave("scalar", ("p", 0, 1), half=1)
        stage1(2, 1)
        interleave("scalar", ("w1", 0, 2))
        quantise((("p", 0, 1), 1), (("w1", 0, 0), None), (("p", 0, 0), None))
        stage1(2, 0)
        times_slope(2, 1)
        interleave("gpsimd", ("p", 0, 2), half=1, after=(("w1", 0, 0), None))
        interleave("scalar", ("p", 0, 2), half=0)
        stage1(2, 2)
        interleave("vector", ("w1", 1, 0), quarters=(0, 3))
        copy_h(2, 0)
        quantise((("p", 0, 2), 1), (("p", 0, 1), 0), (("p", 0, 2), 0),
                 (("w1", 0, 1), 0), (("w1", 0, 1), 1), (("w1", 0, 2), None))

        stage1(1, 1)
        interleave("scalar", ("p", 2, 1))
        times_slope(2, 2)
        times_slope_gpsimd(2, 0, 0, after=(("w1", 0, 1), 1))
        stage2(0, 0)
        interleave("scalar", ("w1", 1, 0), quarters=(3, 4))
        interleave("scalar", ("w1", 1, 1))
        times_slope(1, 1)
        times_slope_gpsimd(2, 0, 1)
        stage1(1, 0)
        times_factor(0, LAST_FIRST)
        interleave("scalar", ("w1", 1, 2))
        stage1(1, 2)
        quantise((("w1", 1, 1), None), (("w1", 1, 0), None), (("p", 2, 0), 0),
                 (("p", 2, 1), None), (("p", 2, 0), 1), (("w1", 1, 2), None))
        copy_h(1, 0)
        store_pair(0, 0)
        store_pair(0, 2)
        stage2(0, 1, last_pass_later=True)
        interleave("scalar", ("p", 2, 2))
        times_slope(1, 2)
        times_slope_gpsimd(1, 0, 0, after=(("p", 2, 0), 1))
        interleave("scalar", ("p", 1, 1))

        times_factor(0, (5, 4))
        quantise((("p", 2, 2), None), (("p", 1, 0), 0))
        stage2(2, 0, last_pass_later=True)
        store_pair(0, 4)
        times_factor(0, (7, 6))
        times_slope_gpsimd(1, 0, 1, after=(("p", 2, 2), None))
        interleave("scalar", ("p", 1, 2))
        times_factor(2, (1, 0))
        stage2(2, 1)
        store_pair(0, 6)
        times_factor(2, (3, 2))
        store_pair(2, 0)
        quantise((("p", 1, 1), None), (("p", 1, 0), 1))
        times_factor_gpsimd(2, 6)
        times_factor(2, (5, 4, 7))
        store_pair(2, 2)
        quantise((("p", 1, 2), None))
        stage2(1, 0, last_pass_later=True)
        store_pair(2, 4)
        store_pair(2, 6)
        stage2(1, 1)
        for m in range(7):
            times_factor(1, (m,))
            store_middle(m)
        finish_in_parts(1, 7)
